import numpy as np
import ml_dtypes


def mxq(x, axis, fmt="e4m3"):
    dtype, down = {"e4m3": (ml_dtypes.float8_e4m3fn, 7), "e5m2": (ml_dtypes.float8_e5m2, 14)}[fmt]
    v = np.moveaxis(np.asarray(x, np.float32).astype(ml_dtypes.bfloat16).astype(np.float64), axis, -1)
    blocks = v.reshape(v.shape[:-1] + (-1, 32))
    amax = np.abs(blocks).max(-1, keepdims=True)
    byte = np.maximum(np.where(amax > 0, np.frexp(amax)[1] - 1 + 127, 0) - down, 1)
    scale = np.exp2(byte - 127.0)
    codes = (blocks / scale).astype(np.float32).astype(dtype).astype(np.float64)
    return np.moveaxis((codes * scale).reshape(v.shape), -1, axis)


WIDE = False


def mx_kscale(k):
    if not WIDE:
        return np.ones(k)
    levels = np.array([10, -10, 5, -5, 0])
    if k % 512:
        return np.exp2(np.random.permutation(np.resize(levels, k // 32))).repeat(32)
    a = np.empty((k // 512, 16))
    for p in range(k // 512):
        a[p, :8] = np.random.permutation(np.resize(levels, 8))
        for g in range(8):
            far = levels[np.abs(levels - a[p, g]) >= 10]
            a[p, g + 8] = far[np.random.randint(len(far))]
    return np.exp2(a.ravel()).repeat(32)


def f64(x):
    return np.asarray(x).astype(np.float64)


def striped8(idx):
    return np.concatenate([v.reshape(-1, 16).T for v in idx]).astype(np.uint16)


def unstriped8(offs):
    return np.stack([offs[16 * g:16 * g + 16].T.reshape(-1) for g in range(8)]).astype(np.int64)


E2M1 = np.array([0.0, 0.5, 1.0, 1.5, 2.0, 3.0, 4.0, 6.0, -0.0, -0.5, -1.0, -1.5, -2.0, -3.0, -4.0, -6.0])


def pack_weight(w, fmt):
    k, n = w.shape
    w = f64(np.asarray(w, np.float32).astype(ml_dtypes.bfloat16)).reshape(k // 32, 32, n)
    amax = np.abs(w).max(1)
    if fmt == "e4m3":
        byte = np.frexp(amax)[1] - 1 + 127 - 7
    else:
        mant, ex = np.frexp(amax / 6.0)
        byte = np.where(mant > 0.5, ex, ex - 1) + 127
    byte = np.clip(np.where(amax > 0, byte, 1), 1, 254)
    scaled = (w * np.exp2(127.0 - byte)[:, None, :]).reshape(k, n).astype(np.float32)
    by_word = np.ascontiguousarray(scaled.reshape(k // 512, 128, 4, n).transpose(0, 1, 3, 2))
    if fmt == "e4m3":
        words = by_word.astype(ml_dtypes.float8_e4m3fn).view(np.uint8)
    else:
        c = by_word.astype(ml_dtypes.float4_e2m1fn).view(np.uint8) & 0xF
        words = (c[..., 0::2] | (c[..., 1::2] << 4)).reshape(k // 512, 128, 2 * n)
    return np.ascontiguousarray(words), np.ascontiguousarray(byte.astype(np.uint8).reshape(k // 512, 16, n))


def unpack_weight(words, scales, fmt):
    g, _, n = scales.shape
    words = np.ascontiguousarray(words).reshape(g, 128, n, -1)
    if fmt == "e4m3":
        vals = words.view(ml_dtypes.float8_e4m3fn).astype(np.float64)
    else:
        nib = np.empty((g, 128, n, 4), np.uint8)
        nib[..., 0::2] = words & 0xF
        nib[..., 1::2] = words >> 4
        vals = E2M1[nib]
    vals = vals * np.repeat(np.exp2(scales.astype(np.float64) - 127.0), 8, axis=1)[..., None]
    return vals.transpose(0, 1, 3, 2).reshape(g * 512, n)


def silu(v):
    return v / (1.0 + np.exp(-np.maximum(v, -700.0)))


K, M, T, S = 2048, 512, 4096, 2048


def setup_inputs():
    n = np.random.standard_normal
    s = mx_kscale(K)[:, None]
    w = n((K, M)) / np.sqrt(K) / s
    p_w8 = pack_weight(w[:512], "e4m3")
    p_w4 = pack_weight(w[512:], "e2m1")
    return {
        "x": (n((K, S)) * s).astype(np.float32),
        "w8_words": p_w8[0],
        "w8_scales": p_w8[1],
        "w4_words": p_w4[0],
        "w4_scales": p_w4[1],
        "b": (0.3 * n(512)).astype(np.float32),
        "wgo": np.repeat(np.random.uniform(0.5, 2.0, (8, S)), 16, axis=0).astype(np.float32),
        "offs": striped8(np.stack([np.random.permutation(T)[:S] for _ in range(8)])),
    }


def reference(x, w8_words, w8_scales, w4_words, w4_scales, b, wgo, offs):
    x_ = mxq(f64(x), 0, "e4m3")
    w8_ = unpack_weight(w8_words, w8_scales, "e4m3")
    w4_ = unpack_weight(w4_words, w4_scales, "e2m1")
    y = w8_.T @ x_[:512] + w4_.T @ x_[512:]
    place = unstriped8(offs)[np.arange(M) % 128 // 16]
    out = np.zeros((M, T))
    out[np.arange(M)[:, None], place] = f64(wgo)[np.arange(M) % 128] * (silu(y + f64(b)[:, None]))
    return out

@@ -1,0 +1,182 @@
+from contextlib import ExitStack
+
+import concourse.mybir as mybir
+
+K, M, T, S = 2048, 512, 4096, 2048
+FLOPS = 2 * K * M * S
+
+F32 = mybir.dt.float32
+BF16 = mybir.dt.bfloat16
+I32 = mybir.dt.int32
+U32 = mybir.dt.uint32
+U16 = mybir.dt.uint16
+U8 = mybir.dt.uint8
+FP8X4 = mybir.dt.float8_e4m3fn_x4
+FP4X4 = mybir.dt.float4_e2m1fn_x4
+SILU = mybir.ActivationFunctionType.Silu
+MULT = mybir.AluOpType.mult
+
+P = 128
+PACK = 4
+K_PASS = P * PACK
+PASSES = K // K_PASS
+ROW_TILES = M // P
+HALF = S // 2
+PIECE = 512
+PIECES = HALF // PIECE
+LIST_ROWS = 16
+VECTOR_COLS = 320
+
+
+def tile_list_hscat_o_silu_kernel(tc, x, w8_words, w8_scales, w4_words, w4_scales, b, wgo, offs, out):
+    nc = tc.nc
+    with ExitStack() as ctx:
+        held = ctx.enter_context(tc.tile_pool(name="held", bufs=1))
+        raw_pool = ctx.enter_context(tc.tile_pool(name="raw", bufs=1))
+        grouped_pool = ctx.enter_context(tc.tile_pool(name="grouped", bufs=8))
+        code_pool = ctx.enter_context(tc.tile_pool(name="codes", bufs=8))
+        act_pool = ctx.enter_context(tc.tile_pool(name="act", bufs=1))
+        psum = ctx.enter_context(tc.psum_pool(name="psum", bufs=1))
+
+        offsets = held.tile([P, S // LIST_ROWS], U16, name="offsets")
+        w_scales = held.tile([P, PASSES, M], U8, name="w_scales", align_bytes=64)
+        w8 = held.tile([P, PACK * M], U8, name="w8", align_bytes=64)
+        w4 = held.tile([P, PASSES - 1, 2 * M], U8, name="w4", align_bytes=64)
+        bias = held.tile([P, ROW_TILES], F32, name="bias")
+        gates = [held.tile([P, HALF], F32, name=f"gates{h}") for h in range(2)]
+        windows = [held.tile([P, T], F32, name=f"window{m}") for m in range(ROW_TILES)]
+        warm_in = held.tile([P, 8], F32, name="warm_in")
+        warm_out = held.tile([P, 8], F32, name="warm_out")
+
+        nc.gpsimd.memset(w_scales[:].rearrange("p a n -> p (a n)").bitcast(I32), 0)
+        nc.gpsimd.memset(warm_in[:], 0.0)
+        nc.scalar.activation(warm_out[:], warm_in[:], SILU)
+        for m in range(ROW_TILES):
+            if m % 2 == 0:
+                nc.vector.memset(windows[m][:, 0 : T // 2 - 1], 0.0)
+                nc.vector.memset(windows[m][:, T // 2 - 1 : T], 0.0)
+            else:
+                nc.gpsimd.memset(windows[m][:], 0.0)
+
+        w8_rows = w8_words[0].rearrange("p n t -> p (n t)")
+        w4_rows = w4_words.rearrange("a p n -> p a n")
+
+        def load_x(h, a, split):
+            raw = raw_pool.tile([P, PACK * HALF], F32, name=f"raw{a}")
+            rows = x[a * K_PASS : (a + 1) * K_PASS, :].rearrange("(p t) j -> p t j", t=PACK)
+            if split:
+                views = []
+                for c in range(PIECES):
+                    view = raw[:, c * PACK * PIECE : (c + 1) * PACK * PIECE].rearrange("p (t j) -> p t j", t=PACK)
+                    j0 = h * HALF + c * PIECE
+                    nc.sync.dma_start(view, rows[:, :, j0 : j0 + PIECE])
+                    views.append(view)
+                return views
+            view = raw[:].rearrange("p (t j) -> p t j", t=PACK)
+            nc.sync.dma_start(view, rows[:, :, h * HALF : (h + 1) * HALF])
+            return [view[:, :, c * PIECE : (c + 1) * PIECE] for c in range(PIECES)]
+
+        def load_scales(dst_passes, src):
+            for q in range(4):
+                nc.sync.dma_start(
+                    w_scales[32 * q : 32 * q + 4, dst_passes, :].bitcast(I32),
+                    src[:, 4 * q : 4 * q + 4, :].rearrange("a r n -> r a n").bitcast(I32),
+                )
+
+        def interleave(src, vector_cols):
+            grouped = grouped_pool.tile([P, PIECE, PACK], BF16, name="grouped", align_bytes=64)
+            for engine, cols in (("vector", slice(0, vector_cols)), ("scalar", slice(vector_cols, PIECE))):
+                if cols.stop > cols.start:
+                    dst = grouped[:, cols, :].rearrange("p (c i) t -> p c t i", i=4)
+                    part = src[:, :, cols].rearrange("p t (c i) -> p c t i", i=4)
+                    if engine == "vector":
+                        nc.vector.tensor_copy(dst, part)
+                    else:
+                        nc.scalar.copy(dst, part)
+            return grouped
+
+        def quantize(grouped):
+            codes = code_pool.tile([P, PIECE], U32, name="codes", align_bytes=64)
+            scales = code_pool.tile([P, PIECE], U8, name="scales", align_bytes=64)
+            nc.vector.quantize_mx(codes[:].bitcast(FP8X4), scales[:], grouped[:].rearrange("p j t -> p (j t)"))
+            return codes, scales
+
+        def weights(a, m):
+            if a == 0:
+                return w8[:, PACK * P * m : PACK * P * (m + 1)].bitcast(FP8X4)
+            return w4[:, a - 1, 2 * P * m : 2 * P * (m + 1)].bitcast(FP4X4)
+
+        def multiply(acc, a, m, operand):
+            codes, scales = operand
+            nc.tensor.matmul_mx(
+                acc[:],
+                lhsT=weights(a, m),
+                lhsT_scale=w_scales[:, a, m * P : (m + 1) * P],
+                rhs=codes[:].bitcast(FP8X4),
+                rhs_scale=scales[:],
+                start=(a == 0),
+                stop=(a == PASSES - 1),
+            )
+
+        def activate(act, accs, m):
+            for c in range(PIECES):
+                nc.scalar.activation(act[:, c * PIECE : (c + 1) * PIECE], accs[c][:], SILU, bias=bias[:, m : m + 1])
+            return act
+
+        def scatter(act, m, h):
+            cols = HALF // LIST_ROWS
+            nc.vector.tensor_tensor(windows[m][:].indirect(offsets[:, h * cols : (h + 1) * cols]), act[:], gates[h][:], MULT)
+
+        raw0 = [load_x(0, 0, False)]
+        load_scales(slice(0, 1), w8_scales)
+        nc.sync.dma_start(w8[:].bitcast(I32), w8_rows.bitcast(I32))
+        nc.sync.dma_start(w4[:].bitcast(I32), w4_rows.bitcast(I32))
+        raw0.append(load_x(0, 1, False))
+        load_scales(slice(1, PASSES), w4_scales)
+        raw0.append(load_x(0, 2, False))
+        with nc.allow_non_contiguous_dma(reason="one bias value to a partition"):
+            nc.sync.dma_start(bias[:], b.rearrange("(m p) -> p m", p=P))
+        nc.sync.dma_start(offsets[:], offs)
+        raw0.append(load_x(0, 3, True))
+        nc.sync.dma_start(gates[0][:], wgo[:, 0:HALF])
+
+        accs0 = [[psum.tile([P, PIECE], F32, name=f"acc{m}_{c}") for c in range(PIECES)] for m in range(ROW_TILES)]
+        operands0 = []
+        for a in range(PASSES):
+            if a < PASSES - 1:
+                shares = (PIECE, 0)
+            else:
+                shares = (VECTOR_COLS, VECTOR_COLS)
+            groups = [interleave(raw0[a][c], shares[c]) for c in range(PIECES)]
+            operands0.append([quantize(g) for g in groups])
+            for c in range(PIECES):
+                for m in range(ROW_TILES):
+                    multiply(accs0[m][c], a, m, operands0[a][c])
+        early = [act_pool.tile([P, HALF], F32, name=f"act{m}") for m in range(2)]
+        for m in range(2):
+            scatter(activate(early[m][:], accs0[m], m), m, 0)
+
+        raw1 = [load_x(1, a, a in (0, PASSES - 1)) for a in range(PASSES)]
+        nc.sync.dma_start(gates[1][:], wgo[:, HALF:S])
+        accs1 = [[psum.tile([P, PIECE], F32, name=f"acc{m}_{c}") for c in range(PIECES)] for m in range(2)]
+        operands1 = []
+        lates = []
+        for a in range(PASSES):
+            groups = [interleave(raw1[a][c], 0) for c in range(PIECES)]
+            operands1.append([quantize(g) for g in groups])
+            for m in range(len(accs1)):
+                for c in range(PIECES):
+                    multiply(accs1[m][c], a, m, operands1[a][c])
+            if a % 2 == 1:
+                m = len(accs1)
+                late = raw_pool.tile([P, ROW_TILES, HALF], F32, name="late", tag=f"raw{a}")
+                lates.append(late)
+                scatter(activate(late[:, 0, :], accs0[m], m), m, 0)
+                accs1.append([psum.tile([P, PIECE], F32, name=f"acc{m}_{c}") for c in range(PIECES)])
+                for c in range(PIECES):
+                    for done in range(a + 1):
+                        multiply(accs1[m][c], done, m, operands1[done][c])
+        for m in range(ROW_TILES):
+            act = lates[1][:, m + 1, :] if m + 1 < ROW_TILES else lates[0][:, 1, :]
+            scatter(activate(act, accs1[m], m), m, 1)
+            nc.sync.dma_start(out[m * P : (m + 1) * P, :], windows[m][:])

@@ -20,12 +20,15 @@ P = 128
 PACK = 4
 K_PASS = P * PACK
 PASSES = K // K_PASS
+LAST = PASSES - 1
 ROW_TILES = M // P
 HALF = S // 2
 PIECE = 512
-PIECES = HALF // PIECE
+NARROW = 128
 LIST_ROWS = 16
 VECTOR_COLS = 320
+EARLY_TILES = 2
+EARLY_ROWS = EARLY_TILES * P
 
 
 def tile_list_hscat_o_silu_kernel(tc, x, w8_words, w8_scales, w4_words, w4_scales, b, wgo, offs, out):
@@ -33,48 +36,43 @@ def tile_list_hscat_o_silu_kernel(tc, x, w8_words, w8_scales, w4_words, w4_scale
     with ExitStack() as ctx:
         held = ctx.enter_context(tc.tile_pool(name="held", bufs=1))
         raw_pool = ctx.enter_context(tc.tile_pool(name="raw", bufs=1))
-        grouped_pool = ctx.enter_context(tc.tile_pool(name="grouped", bufs=8))
-        code_pool = ctx.enter_context(tc.tile_pool(name="codes", bufs=8))
-        act_pool = ctx.enter_context(tc.tile_pool(name="act", bufs=1))
+        grouped_pool = ctx.enter_context(tc.tile_pool(name="grouped", bufs=1))
+        code_pool = ctx.enter_context(tc.tile_pool(name="codes", bufs=1))
         psum = ctx.enter_context(tc.psum_pool(name="psum", bufs=1))
 
         offsets = held.tile([P, S // LIST_ROWS], U16, name="offsets")
         w_scales = held.tile([P, PASSES, M], U8, name="w_scales", align_bytes=64)
-        w8 = held.tile([P, PACK * M], U8, name="w8", align_bytes=64)
-        w4 = held.tile([P, PASSES - 1, 2 * M], U8, name="w4", align_bytes=64)
+        w8_first = held.tile([P, PACK * EARLY_ROWS], U8, name="w8_first", align_bytes=64)
+        w8_rest = held.tile([P, PACK * (M - EARLY_ROWS)], U8, name="w8_rest", align_bytes=64)
+        w4_first = held.tile([P, PASSES - 1, 2 * EARLY_ROWS], U8, name="w4_first", align_bytes=64)
+        w4_rest = held.tile([P, PASSES - 1, 2 * (M - EARLY_ROWS)], U8, name="w4_rest", align_bytes=64)
         bias = held.tile([P, ROW_TILES], F32, name="bias")
-        gates = [held.tile([P, HALF], F32, name=f"gates{h}") for h in range(2)]
+        gates = [held.tile([P, HALF], F32, name="gates0")]
         windows = [held.tile([P, T], F32, name=f"window{m}") for m in range(ROW_TILES)]
+        early = [held.tile([P, HALF], F32, name=f"early{m}") for m in range(2)]
         warm_in = held.tile([P, 8], F32, name="warm_in")
         warm_out = held.tile([P, 8], F32, name="warm_out")
 
-        nc.gpsimd.memset(w_scales[:].rearrange("p a n -> p (a n)").bitcast(I32), 0)
-        nc.gpsimd.memset(warm_in[:], 0.0)
+        nc.vector.memset(warm_in[:], 0.0)
         nc.scalar.activation(warm_out[:], warm_in[:], SILU)
+        nc.vector.memset(w_scales[:].rearrange("p a n -> p (a n)").bitcast(I32), 0)
         for m in range(ROW_TILES):
-            if m % 2 == 0:
-                nc.vector.memset(windows[m][:, 0 : T // 2 - 1], 0.0)
-                nc.vector.memset(windows[m][:, T // 2 - 1 : T], 0.0)
-            else:
-                nc.gpsimd.memset(windows[m][:], 0.0)
+            (nc.vector if m < 2 else nc.gpsimd).memset(windows[m][:], 0.0)
 
         w8_rows = w8_words[0].rearrange("p n t -> p (n t)")
         w4_rows = w4_words.rearrange("a p n -> p a n")
 
-        def load_x(h, a, split):
+        def load_x(h, a, widths):
             raw = raw_pool.tile([P, PACK * HALF], F32, name=f"raw{a}")
             rows = x[a * K_PASS : (a + 1) * K_PASS, :].rearrange("(p t) j -> p t j", t=PACK)
-            if split:
-                views = []
-                for c in range(PIECES):
-                    view = raw[:, c * PACK * PIECE : (c + 1) * PACK * PIECE].rearrange("p (t j) -> p t j", t=PACK)
-                    j0 = h * HALF + c * PIECE
-                    nc.sync.dma_start(view, rows[:, :, j0 : j0 + PIECE])
-                    views.append(view)
-                return views
-            view = raw[:].rearrange("p (t j) -> p t j", t=PACK)
-            nc.sync.dma_start(view, rows[:, :, h * HALF : (h + 1) * HALF])
-            return [view[:, :, c * PIECE : (c + 1) * PIECE] for c in range(PIECES)]
+            views = []
+            j0 = 0
+            for width in widths:
+                view = raw[:, PACK * j0 : PACK * (j0 + width)].rearrange("p (t j) -> p t j", t=PACK)
+                nc.sync.dma_start(view, rows[:, :, h * HALF + j0 : h * HALF + j0 + width])
+                views += [view[:, :, c : c + min(width, PIECE)] for c in range(0, width, PIECE)]
+                j0 += width
+            return views
 
         def load_scales(dst_passes, src):
             for q in range(4):
@@ -83,100 +81,139 @@ def tile_list_hscat_o_silu_kernel(tc, x, w8_words, w8_scales, w4_words, w4_scale
                     src[:, 4 * q : 4 * q + 4, :].rearrange("a r n -> r a n").bitcast(I32),
                 )
 
-        def interleave(src, vector_cols):
-            grouped = grouped_pool.tile([P, PIECE, PACK], BF16, name="grouped", align_bytes=64)
-            for engine, cols in (("vector", slice(0, vector_cols)), ("scalar", slice(vector_cols, PIECE))):
+        def interleave(src, vector_cols, slot):
+            width = src.shape[2]
+            grouped = grouped_pool.tile([P, width, PACK], BF16, name=f"grouped{slot}", align_bytes=64)
+            for on_vector, cols in ((True, slice(0, vector_cols)), (False, slice(vector_cols, width))):
                 if cols.stop > cols.start:
-                    dst = grouped[:, cols, :].rearrange("p (c i) t -> p c t i", i=4)
-                    part = src[:, :, cols].rearrange("p t (c i) -> p c t i", i=4)
-                    if engine == "vector":
+                    dst = grouped[:, cols, :].rearrange("p (c i) t -> p c t i", i=2)
+                    part = src[:, :, cols].rearrange("p t (c i) -> p c t i", i=2)
+                    if on_vector:
                         nc.vector.tensor_copy(dst, part)
                     else:
                         nc.scalar.copy(dst, part)
             return grouped
 
-        def quantize(grouped):
-            codes = code_pool.tile([P, PIECE], U32, name="codes", align_bytes=64)
-            scales = code_pool.tile([P, PIECE], U8, name="scales", align_bytes=64)
-            nc.vector.quantize_mx(codes[:].bitcast(FP8X4), scales[:], grouped[:].rearrange("p j t -> p (j t)"))
+        def new_operand(a, c):
+            codes = code_pool.tile([P, PIECE], U32, name=f"codes{a}_{c}", align_bytes=64)
+            scales = code_pool.tile([P, PIECE], U8, name=f"scales{a}_{c}", align_bytes=64)
             return codes, scales
 
-        def weights(a, m):
-            if a == 0:
-                return w8[:, PACK * P * m : PACK * P * (m + 1)].bitcast(FP8X4)
-            return w4[:, a - 1, 2 * P * m : 2 * P * (m + 1)].bitcast(FP4X4)
+        def quantize(operand, cols, grouped):
+            codes, scales = operand
+            nc.vector.quantize_mx(codes[:, cols].bitcast(FP8X4), scales[:, cols], grouped[:].rearrange("p j t -> p (j t)"))
 
-        def multiply(acc, a, m, operand):
+        def weights(a, m):
+            w8, w4 = (w8_first, w4_first) if m < EARLY_TILES else (w8_rest, w4_rest)
+            i = m % EARLY_TILES
+            if a == 0:
+                return w8[:, PACK * P * i : PACK * P * (i + 1)].bitcast(FP8X4)
+            return w4[:, a - 1, 2 * P * i : 2 * P * (i + 1)].bitcast(FP4X4)
+
+        def multiply(acc, a, m, operand, cols, start, stop):
             codes, scales = operand
             nc.tensor.matmul_mx(
                 acc[:],
                 lhsT=weights(a, m),
                 lhsT_scale=w_scales[:, a, m * P : (m + 1) * P],
-                rhs=codes[:].bitcast(FP8X4),
-                rhs_scale=scales[:],
-                start=(a == 0),
-                stop=(a == PASSES - 1),
+                rhs=codes[:, cols].bitcast(FP8X4),
+                rhs_scale=scales[:, cols],
+                start=start,
+                stop=stop,
             )
 
-        def activate(act, accs, m):
-            for c in range(PIECES):
-                nc.scalar.activation(act[:, c * PIECE : (c + 1) * PIECE], accs[c][:], SILU, bias=bias[:, m : m + 1])
-            return act
+        def bank(number, width=PIECE):
+            return psum.tile([P, width], F32, name=f"bank{number}")
+
+        def activate(act, acc, m):
+            nc.scalar.activation(act, acc[:], SILU, bias=bias[:, m : m + 1])
 
         def scatter(act, m, h):
             cols = HALF // LIST_ROWS
-            nc.vector.tensor_tensor(windows[m][:].indirect(offsets[:, h * cols : (h + 1) * cols]), act[:], gates[h][:], MULT)
+            nc.vector.tensor_tensor(windows[m][:].indirect(offsets[:, h * cols : (h + 1) * cols]), act, gates[h][:], MULT)
 
-        raw0 = [load_x(0, 0, False)]
+        whole = slice(0, PIECE)
+
+        raw0 = [load_x(0, a, [HALF]) for a in range(2)]
         load_scales(slice(0, 1), w8_scales)
-        nc.sync.dma_start(w8[:].bitcast(I32), w8_rows.bitcast(I32))
-        nc.sync.dma_start(w4[:].bitcast(I32), w4_rows.bitcast(I32))
-        raw0.append(load_x(0, 1, False))
+        nc.sync.dma_start(w8_first[:].bitcast(I32), w8_rows[:, 0 : PACK * EARLY_ROWS].bitcast(I32))
+        nc.sync.dma_start(w4_first[:].bitcast(I32), w4_rows[:, :, 0 : 2 * EARLY_ROWS].bitcast(I32))
+        raw0.append(load_x(0, 2, [HALF]))
         load_scales(slice(1, PASSES), w4_scales)
-        raw0.append(load_x(0, 2, False))
         with nc.allow_non_contiguous_dma(reason="one bias value to a partition"):
             nc.sync.dma_start(bias[:], b.rearrange("(m p) -> p m", p=P))
         nc.sync.dma_start(offsets[:], offs)
-        raw0.append(load_x(0, 3, True))
+        raw0.append(load_x(0, LAST, [PIECE, PIECE // 2, PIECE // 2]))
         nc.sync.dma_start(gates[0][:], wgo[:, 0:HALF])
+        nc.sync.dma_start(w8_rest[:].bitcast(I32), w8_rows[:, PACK * EARLY_ROWS :].bitcast(I32))
+        nc.sync.dma_start(w4_rest[:].bitcast(I32), w4_rows[:, :, 2 * EARLY_ROWS :].bitcast(I32))
 
-        accs0 = [[psum.tile([P, PIECE], F32, name=f"acc{m}_{c}") for c in range(PIECES)] for m in range(ROW_TILES)]
-        operands0 = []
-        for a in range(PASSES):
-            if a < PASSES - 1:
-                shares = (PIECE, 0)
-            else:
-                shares = (VECTOR_COLS, VECTOR_COLS)
-            groups = [interleave(raw0[a][c], shares[c]) for c in range(PIECES)]
-            operands0.append([quantize(g) for g in groups])
-            for c in range(PIECES):
-                for m in range(ROW_TILES):
-                    multiply(accs0[m][c], a, m, operands0[a][c])
-        early = [act_pool.tile([P, HALF], F32, name=f"act{m}") for m in range(2)]
-        for m in range(2):
-            scatter(activate(early[m][:], accs0[m], m), m, 0)
+        wide_acc = bank(0)
+        narrow_accs = [bank(1 + q, NARROW) for q in range(PIECE // NARROW)]
+        accs01 = [bank(5), bank(6)]
+        operands0 = [[new_operand(a, c) for c in range(2)] for a in range(PASSES)]
+        for a in range(LAST):
+            shares = (PIECE if a == LAST - 1 else 0, 0)
+            groups = [interleave(raw0[a][c], shares[c], 2 * a + c) for c in range(2)]
+            quantize(operands0[a][0], whole, groups[0])
+            multiply(wide_acc, a, 0, operands0[a][0], whole, a == 0, False)
+            quantize(operands0[a][1], whole, groups[1])
+            for q, acc in enumerate(narrow_accs):
+                multiply(acc, a, 0, operands0[a][1], slice(q * NARROW, (q + 1) * NARROW), a == 0, False)
+            for c in range(2):
+                multiply(accs01[c], a, 1, operands0[a][c], whole, a == 0, False)
+        quantize(operands0[LAST][0], whole, interleave(raw0[LAST][0], VECTOR_COLS, 2 * LAST))
+        multiply(wide_acc, LAST, 0, operands0[LAST][0], whole, False, True)
+        activate(early[0][:, 0:PIECE], wide_acc, 0)
+        for part in range(2):
+            cols = slice(part * PIECE // 2, (part + 1) * PIECE // 2)
+            quantize(operands0[LAST][1], cols, interleave(raw0[LAST][1 + part], PIECE // 2, 2 * LAST + 1 + part))
+            for q in (2 * part, 2 * part + 1):
+                multiply(narrow_accs[q], LAST, 0, operands0[LAST][1], slice(q * NARROW, (q + 1) * NARROW), False, True)
+                activate(early[0][:, PIECE + q * NARROW : PIECE + (q + 1) * NARROW], narrow_accs[q], 0)
+        scatter(early[0][:], 0, 0)
+        for c in range(2):
+            multiply(accs01[c], LAST, 1, operands0[LAST][c], whole, False, True)
+            activate(early[1][:, c * PIECE : (c + 1) * PIECE], accs01[c], 1)
+        scatter(early[1][:], 1, 0)
 
-        raw1 = [load_x(1, a, a in (0, PASSES - 1)) for a in range(PASSES)]
+        def product0(m, c, number):
+            acc = bank(number)
+            for a in reversed(range(PASSES)):
+                multiply(acc, a, m, operands0[a][c], whole, a == LAST, a == 0)
+            return acc
+
+        accs0 = {2: (product0(2, 0, 4), product0(2, 1, 3)), 3: (product0(3, 0, 6), product0(3, 1, 7))}
+
+        raw1 = [load_x(1, a, [PIECE, PIECE]) for a in range(PASSES)]
+        gates.append(held.tile([P, HALF], F32, name="gates1", tag="early0"))
         nc.sync.dma_start(gates[1][:], wgo[:, HALF:S])
-        accs1 = [[psum.tile([P, PIECE], F32, name=f"acc{m}_{c}") for c in range(PIECES)] for m in range(2)]
+        banks1 = [(0, 1), (2, 5), (4, 3), (6, 7)]
+        accs1 = [[bank(n) for n in banks1[m]] for m in range(2)]
         operands1 = []
         lates = []
         for a in range(PASSES):
-            groups = [interleave(raw1[a][c], 0) for c in range(PIECES)]
-            operands1.append([quantize(g) for g in groups])
+            groups = [interleave(raw1[a][c], 0, 2 * a + c) for c in range(2)]
+            operands1.append([new_operand(a, c) for c in range(2)])
+            for c in range(2):
+                quantize(operands1[a][c], whole, groups[c])
             for m in range(len(accs1)):
-                for c in range(PIECES):
-                    multiply(accs1[m][c], a, m, operands1[a][c])
+                for c in range(2):
+                    multiply(accs1[m][c], a, m, operands1[a][c], whole, a == 0, a == LAST)
             if a % 2 == 1:
                 m = len(accs1)
                 late = raw_pool.tile([P, ROW_TILES, HALF], F32, name="late", tag=f"raw{a}")
                 lates.append(late)
-                scatter(activate(late[:, 0, :], accs0[m], m), m, 0)
-                accs1.append([psum.tile([P, PIECE], F32, name=f"acc{m}_{c}") for c in range(PIECES)])
-                for c in range(PIECES):
+                for c in range(2):
+                    activate(late[:, 0, c * PIECE : (c + 1) * PIECE], accs0[m][c], m)
+                scatter(late[:, 0, :], m, 0)
+                accs1.append([bank(n) for n in banks1[m]])
+                for c in range(2):
                     for done in range(a + 1):
-                        multiply(accs1[m][c], done, m, operands1[done][c])
+                        multiply(accs1[m][c], done, m, operands1[done][c], whole, done == 0, done == LAST)
         for m in range(ROW_TILES):
             act = lates[1][:, m + 1, :] if m + 1 < ROW_TILES else lates[0][:, 1, :]
-            scatter(activate(act, accs1[m], m), m, 1)
+            for c in range(2):
+                activate(act[:, c * PIECE : (c + 1) * PIECE], accs1[m][c], m)
+            scatter(act, m, 1)
             nc.sync.dma_start(out[m * P : (m + 1) * P, :], windows[m][:])

@@ -46,16 +46,17 @@ def tile_list_hscat_o_silu_kernel(tc, x, w8_words, w8_scales, w4_words, w4_scale
         w8_rest = held.tile([P, PACK * (M - EARLY_ROWS)], U8, name="w8_rest", align_bytes=64)
         w4_first = held.tile([P, PASSES - 1, 2 * EARLY_ROWS], U8, name="w4_first", align_bytes=64)
         w4_rest = held.tile([P, PASSES - 1, 2 * (M - EARLY_ROWS)], U8, name="w4_rest", align_bytes=64)
-        bias = held.tile([P, ROW_TILES], F32, name="bias")
+        bias_first = held.tile([P, EARLY_TILES], F32, name="bias_first")
+        bias_rest = held.tile([P, ROW_TILES - EARLY_TILES], F32, name="bias_rest")
         gates = [held.tile([P, HALF], F32, name="gates0")]
         windows = [held.tile([P, T], F32, name=f"window{m}") for m in range(ROW_TILES)]
         early = [held.tile([P, HALF], F32, name=f"early{m}") for m in range(2)]
         warm_in = held.tile([P, 8], F32, name="warm_in")
         warm_out = held.tile([P, 8], F32, name="warm_out")
 
-        nc.vector.memset(warm_in[:], 0.0)
+        nc.gpsimd.memset(warm_in[:], 0.0)
         nc.scalar.activation(warm_out[:], warm_in[:], SILU)
-        nc.vector.memset(w_scales[:].rearrange("p a n -> p (a n)").bitcast(I32), 0)
+        nc.gpsimd.memset(w_scales[:].rearrange("p a n -> p (a n)").bitcast(I32), 0)
         for m in range(ROW_TILES):
             (nc.vector if m < 2 else nc.gpsimd).memset(windows[m][:], 0.0)
 
@@ -126,7 +127,9 @@ def tile_list_hscat_o_silu_kernel(tc, x, w8_words, w8_scales, w4_words, w4_scale
             return psum.tile([P, width], F32, name=f"bank{number}")
 
         def activate(act, acc, m):
-            nc.scalar.activation(act, acc[:], SILU, bias=bias[:, m : m + 1])
+            bias = bias_first if m < EARLY_TILES else bias_rest
+            i = m % EARLY_TILES
+            nc.scalar.activation(act, acc[:], SILU, bias=bias[:, i : i + 1])
 
         def scatter(act, m, h):
             cols = HALF // LIST_ROWS
@@ -134,19 +137,24 @@ def tile_list_hscat_o_silu_kernel(tc, x, w8_words, w8_scales, w4_words, w4_scale
 
         whole = slice(0, PIECE)
 
-        raw0 = [load_x(0, a, [HALF]) for a in range(2)]
+        def load_bias(dst, rows):
+            with nc.allow_non_contiguous_dma(reason="one bias value to a partition"):
+                nc.sync.dma_start(dst[:], b[rows].rearrange("(m p) -> p m", p=P))
+
+        raw0 = [load_x(0, 0, [HALF])]
         load_scales(slice(0, 1), w8_scales)
         nc.sync.dma_start(w8_first[:].bitcast(I32), w8_rows[:, 0 : PACK * EARLY_ROWS].bitcast(I32))
         nc.sync.dma_start(w4_first[:].bitcast(I32), w4_rows[:, :, 0 : 2 * EARLY_ROWS].bitcast(I32))
-        raw0.append(load_x(0, 2, [HALF]))
+        raw0.append(load_x(0, 1, [HALF]))
         load_scales(slice(1, PASSES), w4_scales)
-        with nc.allow_non_contiguous_dma(reason="one bias value to a partition"):
-            nc.sync.dma_start(bias[:], b.rearrange("(m p) -> p m", p=P))
-        nc.sync.dma_start(offsets[:], offs)
+        raw0.append(load_x(0, 2, [HALF]))
         raw0.append(load_x(0, LAST, [PIECE, PIECE // 2, PIECE // 2]))
+        load_bias(bias_first, slice(0, EARLY_ROWS))
+        nc.sync.dma_start(offsets[:], offs)
         nc.sync.dma_start(gates[0][:], wgo[:, 0:HALF])
         nc.sync.dma_start(w8_rest[:].bitcast(I32), w8_rows[:, PACK * EARLY_ROWS :].bitcast(I32))
         nc.sync.dma_start(w4_rest[:].bitcast(I32), w4_rows[:, :, 2 * EARLY_ROWS :].bitcast(I32))
+        load_bias(bias_rest, slice(EARLY_ROWS, M))
 
         wide_acc = bank(0)
         narrow_accs = [bank(1 + q, NARROW) for q in range(PIECE // NARROW)]
@@ -167,7 +175,7 @@ def tile_list_hscat_o_silu_kernel(tc, x, w8_words, w8_scales, w4_words, w4_scale
         activate(early[0][:, 0:PIECE], wide_acc, 0)
         for part in range(2):
             cols = slice(part * PIECE // 2, (part + 1) * PIECE // 2)
-            quantize(operands0[LAST][1], cols, interleave(raw0[LAST][1 + part], PIECE // 2, 2 * LAST + 1 + part))
+            quantize(operands0[LAST][1], cols, interleave(raw0[LAST][1 + part], (VECTOR_COLS // 2, PIECE // 2)[part], 2 * LAST + 1 + part))
             for q in (2 * part, 2 * part + 1):
                 multiply(narrow_accs[q], LAST, 0, operands0[LAST][1], slice(q * NARROW, (q + 1) * NARROW), False, True)
                 activate(early[0][:, PIECE + q * NARROW : PIECE + (q + 1) * NARROW], narrow_accs[q], 0)
@@ -185,7 +193,7 @@ def tile_list_hscat_o_silu_kernel(tc, x, w8_words, w8_scales, w4_words, w4_scale
 
         accs0 = {2: (product0(2, 0, 4), product0(2, 1, 3)), 3: (product0(3, 0, 6), product0(3, 1, 7))}
 
-        raw1 = [load_x(1, a, [PIECE, PIECE]) for a in range(PASSES)]
+        raw1 = [load_x(1, a, [PIECE, PIECE // 2, PIECE // 2] if a == LAST else [PIECE, PIECE]) for a in range(PASSES)]
         gates.append(held.tile([P, HALF], F32, name="gates1", tag="early0"))
         nc.sync.dma_start(gates[1][:], wgo[:, HALF:S])
         banks1 = [(0, 1), (2, 5), (4, 3), (6, 7)]
@@ -193,10 +201,13 @@ def tile_list_hscat_o_silu_kernel(tc, x, w8_words, w8_scales, w4_words, w4_scale
         operands1 = []
         lates = []
         for a in range(PASSES):
-            groups = [interleave(raw1[a][c], 0, 2 * a + c) for c in range(2)]
+            groups = [interleave(view, 0, 2 * a + i) for i, view in enumerate(raw1[a])]
             operands1.append([new_operand(a, c) for c in range(2)])
-            for c in range(2):
-                quantize(operands1[a][c], whole, groups[c])
+            j0 = 0
+            for grouped in groups:
+                width = grouped.shape[1]
+                quantize(operands1[a][j0 // PIECE], slice(j0 % PIECE, j0 % PIECE + width), grouped)
+                j0 += width
             for m in range(len(accs1)):
                 for c in range(2):
                     multiply(accs1[m][c], a, m, operands1[a][c], whole, a == 0, a == LAST)

from contextlib import ExitStack

import concourse.mybir as mybir

K, M, T, S = 2048, 512, 4096, 2048
FLOPS = 2 * K * M * S

F32 = mybir.dt.float32
BF16 = mybir.dt.bfloat16
I32 = mybir.dt.int32
U32 = mybir.dt.uint32
U16 = mybir.dt.uint16
U8 = mybir.dt.uint8
FP8X4 = mybir.dt.float8_e4m3fn_x4
FP4X4 = mybir.dt.float4_e2m1fn_x4
SILU = mybir.ActivationFunctionType.Silu
MULT = mybir.AluOpType.mult

P = 128
PACK = 4
K_PASS = P * PACK
PASSES = K // K_PASS
LAST = PASSES - 1
ROW_TILES = M // P
HALF = S // 2
PIECE = 512
NARROW = 128
LIST_ROWS = 16
VECTOR_COLS = 320
EARLY_TILES = 2
EARLY_ROWS = EARLY_TILES * P


def tile_list_hscat_o_silu_kernel(tc, x, w8_words, w8_scales, w4_words, w4_scales, b, wgo, offs, out):
    nc = tc.nc
    with ExitStack() as ctx:
        held = ctx.enter_context(tc.tile_pool(name="held", bufs=1))
        raw_pool = ctx.enter_context(tc.tile_pool(name="raw", bufs=1))
        grouped_pool = ctx.enter_context(tc.tile_pool(name="grouped", bufs=1))
        code_pool = ctx.enter_context(tc.tile_pool(name="codes", bufs=1))
        psum = ctx.enter_context(tc.psum_pool(name="psum", bufs=1))

        offsets = held.tile([P, S // LIST_ROWS], U16, name="offsets")
        w_scales = held.tile([P, PASSES, M], U8, name="w_scales", align_bytes=64)
        w8_first = held.tile([P, PACK * EARLY_ROWS], U8, name="w8_first", align_bytes=64)
        w8_rest = held.tile([P, PACK * (M - EARLY_ROWS)], U8, name="w8_rest", align_bytes=64)
        w4_first = held.tile([P, PASSES - 1, 2 * EARLY_ROWS], U8, name="w4_first", align_bytes=64)
        w4_rest = held.tile([P, PASSES - 1, 2 * (M - EARLY_ROWS)], U8, name="w4_rest", align_bytes=64)
        bias_first = held.tile([P, EARLY_TILES], F32, name="bias_first")
        bias_rest = held.tile([P, ROW_TILES - EARLY_TILES], F32, name="bias_rest")
        gates = [held.tile([P, HALF], F32, name="gates0")]
        windows = [held.tile([P, T], F32, name=f"window{m}") for m in range(ROW_TILES)]
        early = [held.tile([P, HALF], F32, name=f"early{m}") for m in range(2)]
        warm_in = held.tile([P, 8], F32, name="warm_in")
        warm_out = held.tile([P, 8], F32, name="warm_out")

        nc.gpsimd.memset(warm_in[:], 0.0)
        nc.scalar.activation(warm_out[:], warm_in[:], SILU)
        nc.gpsimd.memset(w_scales[:].rearrange("p a n -> p (a n)").bitcast(I32), 0)
        for m in range(ROW_TILES):
            (nc.vector if m < 2 else nc.gpsimd).memset(windows[m][:], 0.0)

        w8_rows = w8_words[0].rearrange("p n t -> p (n t)")
        w4_rows = w4_words.rearrange("a p n -> p a n")

        def load_x(h, a, widths):
            raw = raw_pool.tile([P, PACK * HALF], F32, name=f"raw{a}")
            rows = x[a * K_PASS : (a + 1) * K_PASS, :].rearrange("(p t) j -> p t j", t=PACK)
            views = []
            j0 = 0
            for width in widths:
                view = raw[:, PACK * j0 : PACK * (j0 + width)].rearrange("p (t j) -> p t j", t=PACK)
                nc.sync.dma_start(view, rows[:, :, h * HALF + j0 : h * HALF + j0 + width])
                views += [view[:, :, c : c + min(width, PIECE)] for c in range(0, width, PIECE)]
                j0 += width
            return views

        def load_scales(dst_passes, src):
            for q in range(4):
                nc.sync.dma_start(
                    w_scales[32 * q : 32 * q + 4, dst_passes, :].bitcast(I32),
                    src[:, 4 * q : 4 * q + 4, :].rearrange("a r n -> r a n").bitcast(I32),
                )

        def interleave(src, vector_cols, slot):
            width = src.shape[2]
            grouped = grouped_pool.tile([P, width, PACK], BF16, name=f"grouped{slot}", align_bytes=64)
            for on_vector, cols in ((True, slice(0, vector_cols)), (False, slice(vector_cols, width))):
                if cols.stop > cols.start:
                    dst = grouped[:, cols, :].rearrange("p (c i) t -> p c t i", i=2)
                    part = src[:, :, cols].rearrange("p t (c i) -> p c t i", i=2)
                    if on_vector:
                        nc.vector.tensor_copy(dst, part)
                    else:
                        nc.scalar.copy(dst, part)
            return grouped

        def new_operand(a, c):
            codes = code_pool.tile([P, PIECE], U32, name=f"codes{a}_{c}", align_bytes=64)
            scales = code_pool.tile([P, PIECE], U8, name=f"scales{a}_{c}", align_bytes=64)
            return codes, scales

        def quantize(operand, cols, grouped):
            codes, scales = operand
            nc.vector.quantize_mx(codes[:, cols].bitcast(FP8X4), scales[:, cols], grouped[:].rearrange("p j t -> p (j t)"))

        def weights(a, m):
            w8, w4 = (w8_first, w4_first) if m < EARLY_TILES else (w8_rest, w4_rest)
            i = m % EARLY_TILES
            if a == 0:
                return w8[:, PACK * P * i : PACK * P * (i + 1)].bitcast(FP8X4)
            return w4[:, a - 1, 2 * P * i : 2 * P * (i + 1)].bitcast(FP4X4)

        def multiply(acc, a, m, operand, cols, start, stop):
            codes, scales = operand
            nc.tensor.matmul_mx(
                acc[:],
                lhsT=weights(a, m),
                lhsT_scale=w_scales[:, a, m * P : (m + 1) * P],
                rhs=codes[:, cols].bitcast(FP8X4),
                rhs_scale=scales[:, cols],
                start=start,
                stop=stop,
            )

        def bank(number, width=PIECE):
            return psum.tile([P, width], F32, name=f"bank{number}")

        def activate(act, acc, m):
            bias = bias_first if m < EARLY_TILES else bias_rest
            i = m % EARLY_TILES
            nc.scalar.activation(act, acc[:], SILU, bias=bias[:, i : i + 1])

        def scatter(act, m, h):
            cols = HALF // LIST_ROWS
            nc.vector.tensor_tensor(windows[m][:].indirect(offsets[:, h * cols : (h + 1) * cols]), act, gates[h][:], MULT)

        whole = slice(0, PIECE)

        def load_bias(dst, rows):
            with nc.allow_non_contiguous_dma(reason="one bias value to a partition"):
                nc.sync.dma_start(dst[:], b[rows].rearrange("(m p) -> p m", p=P))

        raw0 = [load_x(0, 0, [HALF])]
        load_scales(slice(0, 1), w8_scales)
        nc.sync.dma_start(w8_first[:].bitcast(I32), w8_rows[:, 0 : PACK * EARLY_ROWS].bitcast(I32))
        nc.sync.dma_start(w4_first[:].bitcast(I32), w4_rows[:, :, 0 : 2 * EARLY_ROWS].bitcast(I32))
        raw0.append(load_x(0, 1, [HALF]))
        load_scales(slice(1, PASSES), w4_scales)
        raw0.append(load_x(0, 2, [HALF]))
        raw0.append(load_x(0, LAST, [PIECE, PIECE // 2, PIECE // 2]))
        load_bias(bias_first, slice(0, EARLY_ROWS))
        nc.sync.dma_start(offsets[:], offs)
        nc.sync.dma_start(gates[0][:], wgo[:, 0:HALF])
        nc.sync.dma_start(w8_rest[:].bitcast(I32), w8_rows[:, PACK * EARLY_ROWS :].bitcast(I32))
        nc.sync.dma_start(w4_rest[:].bitcast(I32), w4_rows[:, :, 2 * EARLY_ROWS :].bitcast(I32))
        load_bias(bias_rest, slice(EARLY_ROWS, M))

        wide_acc = bank(0)
        narrow_accs = [bank(1 + q, NARROW) for q in range(PIECE // NARROW)]
        accs01 = [bank(5), bank(6)]
        operands0 = [[new_operand(a, c) for c in range(2)] for a in range(PASSES)]
        for a in range(LAST):
            shares = (PIECE if a == LAST - 1 else 0, 0)
            groups = [interleave(raw0[a][c], shares[c], 2 * a + c) for c in range(2)]
            quantize(operands0[a][0], whole, groups[0])
            multiply(wide_acc, a, 0, operands0[a][0], whole, a == 0, False)
            quantize(operands0[a][1], whole, groups[1])
            for q, acc in enumerate(narrow_accs):
                multiply(acc, a, 0, operands0[a][1], slice(q * NARROW, (q + 1) * NARROW), a == 0, False)
            for c in range(2):
                multiply(accs01[c], a, 1, operands0[a][c], whole, a == 0, False)
        quantize(operands0[LAST][0], whole, interleave(raw0[LAST][0], VECTOR_COLS, 2 * LAST))
        multiply(wide_acc, LAST, 0, operands0[LAST][0], whole, False, True)
        activate(early[0][:, 0:PIECE], wide_acc, 0)
        for part in range(2):
            cols = slice(part * PIECE // 2, (part + 1) * PIECE // 2)
            quantize(operands0[LAST][1], cols, interleave(raw0[LAST][1 + part], (VECTOR_COLS // 2, PIECE // 2)[part], 2 * LAST + 1 + part))
            for q in (2 * part, 2 * part + 1):
                multiply(narrow_accs[q], LAST, 0, operands0[LAST][1], slice(q * NARROW, (q + 1) * NARROW), False, True)
                activate(early[0][:, PIECE + q * NARROW : PIECE + (q + 1) * NARROW], narrow_accs[q], 0)
        scatter(early[0][:], 0, 0)
        for c in range(2):
            multiply(accs01[c], LAST, 1, operands0[LAST][c], whole, False, True)
            activate(early[1][:, c * PIECE : (c + 1) * PIECE], accs01[c], 1)
        scatter(early[1][:], 1, 0)

        def product0(m, c, number):
            acc = bank(number)
            for a in reversed(range(PASSES)):
                multiply(acc, a, m, operands0[a][c], whole, a == LAST, a == 0)
            return acc

        accs0 = {2: (product0(2, 0, 4), product0(2, 1, 3)), 3: (product0(3, 0, 6), product0(3, 1, 7))}

        raw1 = [load_x(1, a, [PIECE, PIECE // 2, PIECE // 2] if a == LAST else [PIECE, PIECE]) for a in range(PASSES)]
        gates.append(held.tile([P, HALF], F32, name="gates1", tag="early0"))
        nc.sync.dma_start(gates[1][:], wgo[:, HALF:S])
        banks1 = [(0, 1), (2, 5), (4, 3), (6, 7)]
        accs1 = [[bank(n) for n in banks1[m]] for m in range(2)]
        operands1 = []
        lates = []
        for a in range(PASSES):
            groups = [interleave(view, 0, 2 * a + i) for i, view in enumerate(raw1[a])]
            operands1.append([new_operand(a, c) for c in range(2)])
            j0 = 0
            for grouped in groups:
                width = grouped.shape[1]
                quantize(operands1[a][j0 // PIECE], slice(j0 % PIECE, j0 % PIECE + width), grouped)
                j0 += width
            for m in range(len(accs1)):
                for c in range(2):
                    multiply(accs1[m][c], a, m, operands1[a][c], whole, a == 0, a == LAST)
            if a % 2 == 1:
                m = len(accs1)
                late = raw_pool.tile([P, ROW_TILES, HALF], F32, name="late", tag=f"raw{a}")
                lates.append(late)
                for c in range(2):
                    activate(late[:, 0, c * PIECE : (c + 1) * PIECE], accs0[m][c], m)
                scatter(late[:, 0, :], m, 0)
                accs1.append([bank(n) for n in banks1[m]])
                for c in range(2):
                    for done in range(a + 1):
                        multiply(accs1[m][c], done, m, operands1[done][c], whole, done == 0, done == LAST)
        for m in range(ROW_TILES):
            act = lates[1][:, m + 1, :] if m + 1 < ROW_TILES else lates[0][:, 1, :]
            for c in range(2):
                activate(act[:, c * PIECE : (c + 1) * PIECE], accs1[m][c], m)
            scatter(act, m, 1)
            nc.sync.dma_start(out[m * P : (m + 1) * P, :], windows[m][:])
